import numpy as np, ml_dtypes
CORES = [25,29,65,69,153,157,193,197]
N = 8
BF = ml_dtypes.bfloat16
W, S, B, M = 4096, 480, 8, 4
def dot(a, x):
    return np.add.reduce(a[:, :, None] * x, axis=1)
def put(w, a, x):
    z = B * np.arange(S) + (dot(a, x) & (B - 1))
    np.put_along_axis(w, z[:, None, :], x, 2)
def pack(b, e, q):
    return {"tab": b.reshape(N, 128, W).astype(np.float32).astype(BF), "res": e.reshape(N, 128, M * S).astype(np.float32).astype(BF), "hw": q.reshape(N, 128, 3).astype(np.float32).astype(BF)}
def parts(rng):
    return rng.integers(0, 256, (N, 8, 16, W)), rng.integers(0, 256, (N, 8, 16, M, S)), rng.integers(0, 256, (N, 8, 16, 3))
def store(b, x, q):
    e = np.array(x)
    for r in range(N):
        w = np.array(b[r])
        for t in range(M):
            if t > 0:
                h = dot(q[r, :, :, 0], x[r, :, :, t - 1])
                if r > 0: h = h + dot(q[r - 1, :, :, 1], x[r - 1, :, :, t])
                e[r, :, :, t] = (x[r, :, :, t] - np.take_along_axis(w, (h & (W - 1))[:, None, :], 2)) & 255
            put(w, q[r, :, :, 2], x[r, :, :, t])
    return e
def plant(rng, goal, code):
    b, x, q = parts(rng)
    q[:, :, 0, 0] = 1; q[:, :, 1, 0] = 128; q[:, :, :2, 2] = 16 * rng.integers(0, 16, (N, 8, 2)); q[:, :, 2, 2] = 1
    for r in range(N):
        for t in range(M):
            rest = dot(q[r, :, 3:, 2], x[r, :, 3:, t])
            x[r, :, 2, t] = B * rng.integers(0, 256 // B, (8, S)) + ((code[r, :, t] - rest) & (B - 1))
            if t + 1 < M:
                d = goal[r, :, t + 1] - dot(q[r, :, 2:, 0], x[r, :, 2:, t])
                if r > 0: d = d - dot(q[r - 1, :, :, 1], x[r - 1, :, :, t + 1])
                d = d & (W - 1); x[r, :, 0, t] = d & 127; x[r, :, 1, t] = d >> 7
    return pack(b, store(b, x, q), q)
def chase(rng, code, lag):
    o = rng.integers(0, S, code.shape); t = np.maximum(np.arange(M)[None, None, :, None] - lag, 0)
    return B * o + code[np.arange(N)[:, None, None, None], np.arange(8)[None, :, None, None], t, o]
def setup_inputs(rng):
    return pack(*parts(rng))
def setup_inputs_fresh(rng):
    code = rng.integers(0, B, (N, 8, M, S)); code = np.where(rng.random((N, 8, 1, S)) < 0.5, code[:, :, :1], code)
    a = rng.permutation(N)[:2]; t = np.arange(M)[None, :, None]
    code[a] = (rng.integers(0, B, (2, 8, 1, S)) + t[None] * (1 + 2 * rng.integers(0, B // 2, (2, 8, 1, S)))) & (B - 1)
    goal = chase(rng, code, rng.integers(1, M, code.shape)); goal[:, ::4, 1:] = B * np.arange(S) + code[:, ::4, :-1]
    goal = np.where(rng.random(code.shape) < 0.1, rng.integers(0, W, code.shape), goal)
    one = np.maximum(t - 1, 0) + np.zeros((8, M, S), np.int64)
    two = np.floor(rng.random((8, M, S)) * np.maximum(t - 1, 1)).astype(np.int64)
    for i, came in ((0, one), (1, two)):
        o = np.argsort(rng.random((8, M, S)), axis=-1)
        goal[a[i]] = B * o + code[a[i]][np.arange(8)[:, None, None], came, o]
    return plant(rng, goal, code)
def setup_inputs_same(rng):
    code = (rng.integers(0, B, (N, 8, 1, S)) + np.arange(M)[None, None, :, None] * rng.integers(1, B, (N, 8, 1, S))) & (B - 1)
    return plant(rng, chase(rng, code, rng.integers(0, 2, code.shape)), code)
def setup_inputs_alike(rng):
    goal = rng.integers(0, W, (N, 8, M, S)); code = rng.integers(0, B, (N, 8, M, S)); p = rng.permutation(8); last = S * B - 1
    goal[:, p[0]] = 0; goal[:, p[1]] = W - 1; goal[:, p[2]] = last; goal[:, p[3]] = S * B if S * B < W else W // 2
    goal[:, p[4]] = np.argsort(rng.random((N, M, W)), axis=-1)[..., :S]
    goal[:, p[5]] = rng.choice(np.array([0, B - 1, B, last]), (N, M, S))
    goal[:, p[6]] = B * np.arange(S) + rng.integers(0, B, (N, M, S))
    code[:, p[0]] = 0; code[:, p[2]] = B - 1; code[:, p[5]] = code[:, p[5], :1]
    goal[rng.integers(0, N)] = (W // 4) * rng.integers(0, 4, (1, M, 1)) + np.argsort(rng.random((8, M, W // 4)), axis=-1)[..., :S]
    return plant(rng, goal, code)
def setup_inputs_ends(rng):
    b, x, q = parts(rng); p = rng.permutation(8)
    q[:, p[0], :, 0] = 0; q[:, p[1], :, 1] = 0; q[:, p[2]] = 255; x[:, p[2]] = 255; q[:, p[3], :, 2] = 0; q[:, p[4]] = 0
    q[:, p[3], :, :2] = rng.integers(200, 256, (N, 16, 2))
    x[:, p[3]] = 255 - np.floor(rng.random((N, 16, M, S)) * rng.integers(56, 257, (N, 1, M, S))).astype(np.int64)
    x[:, p[5]] = 255 * rng.integers(0, 2, (N, 16, M, S))
    b[:, p[6]] = 255; x[:, p[6]] = rng.choice(np.array([0, 1, 254, 255]), (N, 16, M, S))
    x[:, p[7]] = x[:, p[7]] * (rng.random((N, 16, M, S)) < 0.1); q[:, p[7]] = rng.choice(np.array([0, 1, 128, 255]), (N, 16, 3))
    return pack(b, store(b, x, q), q)
def uneven(rng, *shape):
    return np.floor(rng.random(shape) * np.exp2(rng.integers(0, 9, (N, 8, 1) + shape[3:]))).astype(np.int64)
def setup_inputs_spread(rng):
    q = np.floor(rng.random((N, 8, 16, 3)) * np.exp2(rng.integers(0, 9, (N, 8, 16, 3)))).astype(np.int64)
    return pack(uneven(rng, N, 8, 16, W), uneven(rng, N, 8, 16, M, S), q)
def check_inputs(d):
    bad = []
    for k in ("tab", "res", "hw"):
        a = np.asarray(d[k]).astype(np.float32)
        if not np.all((a >= 0) & (a <= 255) & (a == np.floor(a))): bad.append("whole numbers from 0 to 255 in " + k)
    return bad
def reference(tab, res, hw):
    b = tab.astype(np.float32).astype(np.int64).reshape(N, 8, 16, W)
    e = res.astype(np.float32).astype(np.int64).reshape(N, 8, 16, M, S)
    q = hw.astype(np.float32).astype(np.int64).reshape(N, 8, 16, 3)
    y = np.zeros((N, 8, 16, M, S), np.int64)
    for r in range(N):
        w = np.array(b[r])
        for t in range(M):
            x = e[r, :, :, t]
            if t > 0:
                h = dot(q[r, :, :, 0], y[r, :, :, t - 1])
                if r > 0: h = h + dot(q[r - 1, :, :, 1], y[r - 1, :, :, t])
                x = (np.take_along_axis(w, (h & (W - 1))[:, None, :], 2) + x) & 255
            y[r, :, :, t] = x
            put(w, q[r, :, :, 2], x)
    return {"y": y.reshape(N, 128, M * S).astype(np.float32).astype(BF)}

@@ -1,0 +1,339 @@
+from concourse.mybir import AluOpType as A, ActivationFunctionType as F
+
+W, S, M = 4096, 480, 4
+K = S // 16
+ZW = 144
+CH = [(0, 16), (16, 24), (24, 30)]
+
+SCRATCH = {
+    "tabw": ("sbuf", [128, W], "bfloat16"),
+    "rs": ("sbuf", [128, M * S], "bfloat16"),
+    "hws": ("sbuf", [128, 3], "bfloat16"),
+    "z": ("sbuf", [128, 3 * ZW], "bfloat16"),
+    "gm": ("sbuf", [128, 8], "bfloat16"),
+    "idn": ("sbuf", [128, 128], "bfloat16"),
+    "nidn": ("sbuf", [128, 128], "bfloat16"),
+    "p8": ("sbuf", [128, 1], "int32"),
+    "p8b": ("sbuf", [128, 1], "int32"),
+    "a8": ("sbuf", [128, 1], "float32"),
+    "cb": ("sbuf", [128, 64], "int32"),
+    "base": ("sbuf", [128, 64], "int32"),
+    "thr": ("sbuf", [128, 3 * S], "bfloat16"),
+    "sm1": ("sbuf", [128, 2 * S], "bfloat16"),
+    "sm2": ("sbuf", [128, 2 * S], "bfloat16"),
+    "sm3": ("sbuf", [128, 2 * S], "bfloat16"),
+    "xs": ("sbuf", [128, 3 * S], "bfloat16"),
+    "wi": ("sbuf", [128, 96], "int32"),
+    "we2": ("sbuf", [128, K], "float32"),
+    "e1s": ("sbuf", [128, K], "float32"),
+    "e1l": ("sbuf", [128, K], "float32"),
+    "e23": ("sbuf", [128, 2 * K], "float32"),
+    "ue": ("sbuf", [128, K], "float32"),
+    "vt": ("sbuf", [128, 96], "float32"),
+    "ha": ("sbuf", [128, 96], "int32"),
+    "hb": ("sbuf", [128, 96], "int32"),
+    "ho": ("sbuf", [128, 96], "uint16"),
+    "wa": ("sbuf", [128, 96], "int32"),
+    "wb": ("sbuf", [128, 96], "int32"),
+    "wc": ("sbuf", [128, 96], "int32"),
+    "wo": ("sbuf", [128, 96], "uint16"),
+}
+for _t in (1, 2, 3):
+    SCRATCH["bs%d" % _t] = ("sbuf", [128, K], "float32")
+    SCRATCH["bl%d" % _t] = ("sbuf", [128, K], "float32")
+for _n in ("pv", "pw", "pu", "pxa", "pxb", "pe1", "pe2", "pw2"):
+    SCRATCH[_n] = ("psum", [128, 512], "float32")
+
+SEMAPHORES = ["cv", "ca", "cp", "cg", "dr", "dr2", "dh", "dt0", "dt1", "dt2", "dy",
+              "ar0", "ar1", "ar2", "ar3", "sn0", "sn1", "sn2", "sn3"]
+
+
+def relay_for(src, dst, T, topo):
+    if topo.may_write(src, dst):
+        return None
+    cand = [c for c in topo.cores_of(src) if T.rank_of(c) is None and topo.may_write(c, dst)]
+    cand.sort(key=lambda c: topo.die(c) != topo.die(src))
+    return cand[0]
+
+
+def nbits(m):
+    return bin(m).count("1")
+
+
+def rank_program(g, core, T, topo):
+    cores = list(T.cores)
+    n = len(cores)
+    rank = T.rank_of(core)
+    sem = T.sem
+    land = [T.e1l, T.bl1, T.bl2, T.bl3]
+
+    if rank is None:
+        for r in range(n - 1):
+            if relay_for(cores[r], cores[r + 1], T, topo) != core:
+                continue
+            dst = cores[r + 1]
+            rid, pid = topo.addr(dst, core)
+            m_in, m_out = topo.mask(cores[r], core), topo.mask(core, dst)
+            for k in range(4):
+                g.wait_ge(sem["ar%d" % k], nbits(m_in))
+                g.remote_dma(land[k][:], land[k][:], sem["ar%d" % k], sem["sn%d" % k], pid, rid, m_out)
+            for k in range(4):
+                g.wait_ge(sem["sn%d" % k], nbits(m_out))
+        return
+
+    first, last = rank == 0, rank == n - 1
+    Q = {"g": g, "v": g.vector, "a": g.scalar, "p": g.tensor, "s": g.sync}
+    cnt = {"v": 0, "a": 0, "p": 0, "g": 0}
+    seen = {}
+
+    def done(q, inst):
+        inst.then_inc(sem["c" + q], 1)
+        cnt[q] += 1
+        return ("c" + q, cnt[q])
+
+    def need(q, *evs):
+        for name, val in evs:
+            if seen.get((q, name), 0) < val:
+                Q[q].wait_ge(sem[name], val)
+                seen[(q, name)] = val
+
+    V, S_, P = g.vector, g.scalar, g.tensor
+
+    if not last:
+        nxt = relay_for(core, cores[rank + 1], T, topo)
+        nxt = cores[rank + 1] if nxt is None else nxt
+        rid, pid = topo.addr(nxt, core)
+        m_out = topo.mask(core, nxt)
+    if not first:
+        prv = relay_for(cores[rank - 1], core, T, topo)
+        prv = cores[rank - 1] if prv is None else prv
+        n_in = nbits(topo.mask(prv, core))
+
+    def send(k, src):
+        g.remote_dma(land[k][:], src, sem["ar%d" % k], sem["sn%d" % k], pid, rid, m_out)
+
+    lo = [128 * c0 for c0, c1 in CH]
+    hi = lo[1:] + [W]
+    nr = 2 * S if first else M * S
+    g.sync.dma_start(T.rs[:, 0:nr], T.res[:, 0:nr]).then_inc(sem.dr, 16)
+    S_.dma_start(T.hws[:], T.hw[:]).then_inc(sem.dh, 16)
+    S_.dma_start(T.tabw[:, lo[0]:hi[0]], T.tab[:, lo[0]:hi[0]]).then_inc(sem.dt0, 16)
+    g.sync.dma_start(T.tabw[:, lo[1]:hi[1]], T.tab[:, lo[1]:hi[1]]).then_inc(sem.dt1, 16)
+    S_.dma_start(T.tabw[:, lo[2]:hi[2]], T.tab[:, lo[2]:hi[2]]).then_inc(sem.dt2, 16)
+    DR, DH = ("dr", 16), ("dh", 16)
+    DR2 = DR
+    if first:
+        need("s", ("dt1", 16))
+        g.sync.dma_start(T.rs[:, nr:M * S], T.res[:, nr:M * S]).then_inc(sem.dr2, 16)
+        DR2 = ("dr2", 16)
+
+    m_gm = done("v", V.memset(T.gm[:], 1.0))
+    m_z = done("v", V.memset(T.z[:], 0.0))
+    done("v", V.memset(T.idn[:], 1.0))
+    m_id = done("v", V.memset(T.nidn[:], -256.0))
+    i_p = done("g", g.iota(T.p8[:], [[0, 1]], 0, 8))
+    need("g", m_gm)
+    s1 = done("g", g.affine_select(T.gm[:], T.gm[:], [[-16, 8]], A.is_ge, 0.0, 0, 1))
+    for c0, c1 in CH:
+        done("g", g.iota(T.cb[:, c0:c1], [[128, c1 - c0]], 0, 0))
+    done("g", g.iota(T.cb[:, K:32], [[0, 32 - K]], 0, 0))
+    i_cb = done("g", g.iota(T.cb[:, 32:64], [[128, 32]], 0, 0))
+    need("g", s1)
+    s_gm = done("g", g.affine_select(T.gm[:], T.gm[:], [[16, 8]], A.is_ge, 0.0, 15, -1))
+    need("g", m_id)
+    done("g", g.affine_select(T.idn[:], T.idn[:], [[-1, 128]], A.is_equal, 0.0, 0, 1))
+    s_id = done("g", g.affine_select(T.nidn[:], T.nidn[:], [[-1, 128]], A.is_equal, 0.0, 0, 1))
+    need("v", i_p)
+    k1 = done("v", V.tensor_scalar(T.p8b[:], T.p8[:], 127, None, A.bitwise_and))
+    need("v", k1)
+    k2 = done("v", V.tensor_copy(T.a8[:], T.p8b[:]))
+    need("v", k2, i_cb)
+    k_base = done("v", V.tensor_scalar(T.base[:], T.cb[:], T.a8[:], None, A.add))
+    ZU, ZV, ZWW = 0, ZW, 2 * ZW
+    need("v", m_z, s_gm, DH)
+    z_w = done("v", V.tensor_scalar(T.z[:, ZWW + 15:ZWW + 143:16], T.gm[:], T.hws[:, 2:3], -256.0, A.mult, A.mult))
+    z_u = done("v", V.tensor_scalar(T.z[:, ZU + 15:ZU + 143:16], T.gm[:], T.hws[:, 0:1], None, A.mult))
+    z_v = done("v", V.tensor_scalar(T.z[:, ZV + 15:ZV + 143:16], T.gm[:], T.hws[:, 1:2], -256.0, A.mult, A.mult))
+
+    def hash16(out, zo, buf, c0, cols):
+        for a in range(16):
+            inst = P.matmul(out[:, 0:cols // 16], T.z[:, zo + 15 - a:zo + 143 - a],
+                            buf[:, c0 + a:c0 + cols:16], a == 0, a == 15)
+        return done("p", inst)
+
+    def xbanks(t):
+        if last and t == M - 1:
+            return [(T.pxa, 0, S // 2), (T.pxb, S // 2, S)]
+        return [(T.pxa, 0, S)]
+
+    def xpre(t):
+        for bank, c0, c1 in xbanks(t):
+            P.matmul(bank[:, 0:c1 - c0], T.idn[:], T.rs[:, t * S + c0:t * S + c1], True, False)
+
+    def wlist(t, src_ev, boff):
+        o = 32 * t
+        src = T.wi[:, 0:K] if t == 0 else T.wa[:, o:o + K]
+        need("v", src_ev)
+        e = done("v", V.tensor_scalar(T.wb[:, o:o + K], src, 7, None, A.bitwise_and))
+        need("v", e, k_base)
+        e = done("v", V.tensor_tensor(T.wc[:, o:o + K], T.wb[:, o:o + K], T.base[:, boff:boff + K], A.add))
+        need("v", e)
+        return done("v", V.tensor_copy(T.wo[:, o:o + K], T.wc[:, o:o + K]))
+
+    def hlist(t, ev):
+        o = 32 * (t - 1)
+        need("v", ev)
+        e = done("v", V.tensor_scalar(T.hb[:, o:o + K], T.ha[:, o:o + K], W - 1, None, A.bitwise_and))
+        need("v", e)
+        return done("v", V.tensor_copy(T.ho[:, o:o + K], T.hb[:, o:o + K]))
+
+    R256 = -1.0 / 256.0
+
+    nw = 2 if first else 3
+    need("p", z_w, DR)
+    p_w = hash16(T.pw, ZWW, T.rs, 0, nw * S)
+    need("p", z_u)
+    p_u = hash16(T.pu, ZU, T.rs, 0, S)
+    ev_e23 = None
+    if not last:
+        need("p", z_v)
+        p_e = hash16(T.pe1, ZV, T.rs, S, S if first else 3 * S)
+    need("p", s_id)
+    xpre(1)
+
+    need("a", DR)
+    nt = 1 if first else 3
+    ev_thr = {1: done("a", S_.activation(T.thr[:, 0:nt * S], T.rs[:, S:(1 + nt) * S], F.Identity, 256.0, -1.0))}
+    if not first:
+        ev_thr[2] = ev_thr[3] = ev_thr[1]
+    if not last:
+        need("a", p_e)
+        a_e1 = done("a", S_.activation(T.e1s[:], T.pe1[:, 0:K], F.Identity, 0.0, R256))
+        if not first:
+            ev_e23 = done("a", S_.activation(T.e23[:], T.pe1[:, K:3 * K], F.Identity, 0.0, R256))
+        need("g", a_e1)
+        send(0, T.e1s[:])
+
+    need("v", p_w)
+    w0 = done("v", V.tensor_scalar(T.wi[:, 0:nw * K], T.pw[:, 0:nw * K], R256, None, A.mult))
+    wl = wlist(0, w0, 0)
+    if first:
+        need("v", p_u)
+        hl = hlist(1, done("v", V.tensor_copy(T.ha[:, 0:K], T.pu[:, 0:K])))
+    for i, (c0, c1) in enumerate(CH):
+        need("v", wl, ("dt%d" % i, 16))
+        sc = done("v", V.tensor_copy(T.tabw[:, lo[i]:hi[i]].indirect(T.wo[:, c0:c1]), T.rs[:, 16 * c0:16 * c1]))
+    if not first:
+        need("v", p_u, ("ar0", n_in))
+        ev_ue = done("v", V.tensor_tensor(T.ue[:], T.pu[:, 0:K], T.e1l[:], A.add))
+    we = {1: (T.wi[:, K:2 * K], w0), 2: (T.wi[:, 2 * K:3 * K], w0)}
+
+    ny = [0]
+
+    def store(q, out, src):
+        Q[q].dma_start(out, src).then_inc(sem.dy, 16)
+        ny[0] += 16
+
+    if last:
+        need("s", DR)
+        store("s", T.y[:, 0:S], T.rs[:, 0:S])
+
+    for t in range(1, M):
+        o = 32 * (t - 1)
+        sm = T["sm%d" % t]
+        xt = T.xs[:, (t - 1) * S:t * S]
+        if first:
+            if t > 1:
+                need("v", p_u)
+                hl = hlist(t, done("v", V.tensor_copy(T.ha[:, o:o + K], T.pu[:, 0:K])))
+        else:
+            if t == 1:
+                need("v", ev_ue, ("ar1", n_in))
+                e = V.tensor_tensor(T.ha[:, o:o + K], T.ue[:], T.bl1[:], A.add)
+            else:
+                need("v", p_u, ("ar%d" % t, n_in))
+                e = V.tensor_tensor(T.ha[:, o:o + K], T.pu[:, 0:K], land[t][:], A.add)
+            hl = hlist(t, done("v", e))
+        offs = T.ho[:, o:o + K]
+        need("v", hl, sc, ev_thr[t])
+        g_c = done("v", V.tensor_tensor(sm[:, S:2 * S], T.tabw[:, 0:W].indirect(offs),
+                                        T.thr[:, (t - 1) * S:t * S], A.is_ge))
+        need("a", hl, sc)
+        g_s = done("a", S_.activation(sm[:, 0:S], T.tabw[:, 0:W].indirect(offs), F.Identity, 0.0, R256))
+
+        need("p", g_c, g_s)
+        if not last:
+            p_v = hash16(T.pv, ZV, sm, 0, 2 * S)
+        if t < M - 1:
+            p_w = hash16(T.pw, ZWW, sm, 0, S)
+        p_x = []
+        for bank, c0, c1 in xbanks(t):
+            P.matmul(bank[:, 0:c1 - c0], T.nidn[:], sm[:, c0:c1], False, False)
+            p_x.append(done("p", P.matmul(bank[:, 0:c1 - c0], T.nidn[:], sm[:, S + c0:S + c1], False, True)))
+
+        if not last:
+            need("v", p_v)
+            if t == 1:
+                e = V.tensor_copy(T.vt[:, o:o + K], T.pv[:, K:2 * K])
+            else:
+                need("v", ev_e23)
+                e = V.tensor_tensor(T.vt[:, o:o + K], T.pv[:, K:2 * K], T.e23[:, (t - 2) * K:(t - 1) * K], A.add)
+            need("v", done("v", e))
+            e = done("v", V.tensor_tensor(T["bs%d" % t][:], T.pv[:, 0:K], T.vt[:, o:o + K], A.add))
+            need("g", e)
+            send(t, T["bs%d" % t][:])
+
+        if last and t == M - 1:
+            h = S // 2
+            need("a", p_x[0])
+            ea = done("a", S_.activation(T.xs[:, 2 * S:2 * S + h], T.pxa[:, 0:h], F.Identity))
+            need("v", p_x[1])
+            eb = done("v", V.tensor_copy(T.xs[:, 2 * S + h:3 * S], T.pxb[:, 0:h]))
+            need("a", ea)
+            store("a", T.y[:, t * S:t * S + h], T.xs[:, 2 * S:2 * S + h])
+            need("s", eb)
+            store("s", T.y[:, t * S + h:M * S], T.xs[:, 2 * S + h:3 * S])
+            break
+
+        need("a", p_x[0])
+        ev_x = done("a", S_.activation(xt, T.pxa[:, 0:S], F.Identity))
+        if not last:
+            need("s", ("sn%d" % t, nbits(m_out)))
+            if t == 1:
+                need("s", DR)
+                store("s", T.y[:, 0:S], T.rs[:, 0:S])
+        need("s", ev_x)
+        store("s", T.y[:, t * S:(t + 1) * S], xt)
+        if t == M - 1:
+            break
+
+        need("p", ev_x)
+        p_u = hash16(T.pu, ZU, T.xs, (t - 1) * S, S)
+        if first:
+            need("p", DR2)
+            if t == 1:
+                p_e2 = hash16(T.pe2, ZV, T.rs, 2 * S, 2 * S)
+                p_w2 = hash16(T.pw2, ZWW, T.rs, 2 * S, S)
+        xpre(t + 1)
+        if first:
+            need("a", DR2)
+            ev_thr[t + 1] = done("a", S_.activation(T.thr[:, t * S:(t + 1) * S], T.rs[:, (t + 1) * S:(t + 2) * S],
+                                                    F.Identity, 256.0, -1.0))
+            if t == 1:
+                need("a", p_e2)
+                ev_e23 = done("a", S_.activation(T.e23[:], T.pe2[:, 0:2 * K], F.Identity, 0.0, R256))
+                need("a", p_w2)
+                we[2] = (T.we2[:], done("a", S_.activation(T.we2[:], T.pw2[:, 0:K], F.Identity, 0.0, R256)))
+
+        need("v", p_w, we[t][1])
+        e = done("v", V.tensor_tensor(T.wa[:, 32 * t:32 * t + K], T.pw[:, 0:K], we[t][0], A.add))
+        wl = wlist(t, e, 32)
+        need("v", wl, ev_x)
+        sc = done("v", V.tensor_copy(T.tabw[:, 0:W].indirect(T.wo[:, 32 * t:32 * t + K]), xt))
+
+    need("s", ("dy", ny[0]))
+    for q in ("v", "a", "p", "g"):
+        need("g", ("c" + q, cnt[q]))
+    if not last:
+        for k in range(4):
+            need("g", ("sn%d" % k, nbits(m_out)))

@@ -1,50 +1,56 @@
+from concourse.bass import DstId, RemoteDMATransfer
 from concourse.mybir import AluOpType as A, ActivationFunctionType as F
 
 W, S, M = 4096, 480, 4
-K = S // 16
-ZW = 144
-CH = [(0, 16), (16, 24), (24, 30)]
+PB = 9
+NP = 1 << PB
+K = NP // 16
+K0 = S // 16
+H = NP // 2
+ZW, C0 = 144, 15
+CH = [(0, 16), (16, 26), (26, 30), (30, 32)]
+FIN = [(0, 12), (12, 22), (22, 30)]
+TILES = {"w": (2, 1.0), "vn": (1, -1.0), "u": (0, 1.0), "wn": (2, -1.0),
+         "v256": (1, 256.0), "w256": (2, 256.0)}
 
 SCRATCH = {
-    "tabw": ("sbuf", [128, W], "bfloat16"),
-    "rs": ("sbuf", [128, M * S], "bfloat16"),
+    "tabw": ("sbuf", [128, W + 256], "bfloat16"),
+    "rs": ("sbuf", [128, (M - 1) * S + NP], "bfloat16"),
     "hws": ("sbuf", [128, 3], "bfloat16"),
-    "z": ("sbuf", [128, 3 * ZW], "bfloat16"),
+    "z": ("sbuf", [128, len(TILES) * ZW], "bfloat16"),
+    "zero": ("sbuf", [128, 2 * K], "bfloat16"),
     "gm": ("sbuf", [128, 8], "bfloat16"),
     "idn": ("sbuf", [128, 128], "bfloat16"),
     "nidn": ("sbuf", [128, 128], "bfloat16"),
-    "p8": ("sbuf", [128, 1], "int32"),
-    "p8b": ("sbuf", [128, 1], "int32"),
-    "a8": ("sbuf", [128, 1], "float32"),
-    "cb": ("sbuf", [128, 64], "int32"),
-    "base": ("sbuf", [128, 64], "int32"),
-    "thr": ("sbuf", [128, 3 * S], "bfloat16"),
-    "sm1": ("sbuf", [128, 2 * S], "bfloat16"),
-    "sm2": ("sbuf", [128, 2 * S], "bfloat16"),
-    "sm3": ("sbuf", [128, 2 * S], "bfloat16"),
-    "xs": ("sbuf", [128, 3 * S], "bfloat16"),
-    "wi": ("sbuf", [128, 96], "int32"),
-    "we2": ("sbuf", [128, K], "float32"),
+    "pi": ("sbuf", [128, 4], "int32"),
+    "pf": ("sbuf", [128, 8], "float32"),
+    "cb": ("sbuf", [128, 2 * K], "int32"),
+    "base": ("sbuf", [128, 3 * K], "int32"),
+    "nu": ("sbuf", [128, 24 * K], "int32"),
+    "pl": ("sbuf", [128, 4 * K], "uint16"),
+    "e0p": ("sbuf", [128, NP], "bfloat16"),
+    "thr": ("sbuf", [128, 3 * NP], "bfloat16"),
+    "xs": ("sbuf", [128, 3 * NP], "bfloat16"),
+    "yb": ("sbuf", [128, 3 * NP], "bfloat16"),
     "e1s": ("sbuf", [128, K], "float32"),
-    "e1l": ("sbuf", [128, K], "float32"),
-    "e23": ("sbuf", [128, 2 * K], "float32"),
     "ue": ("sbuf", [128, K], "float32"),
-    "vt": ("sbuf", [128, 96], "float32"),
-    "ha": ("sbuf", [128, 96], "int32"),
-    "hb": ("sbuf", [128, 96], "int32"),
-    "ho": ("sbuf", [128, 96], "uint16"),
-    "wa": ("sbuf", [128, 96], "int32"),
-    "wb": ("sbuf", [128, 96], "int32"),
-    "wc": ("sbuf", [128, 96], "int32"),
-    "wo": ("sbuf", [128, 96], "uint16"),
+    "ha": ("sbuf", [128, 3 * K], "int32"),
+    "hb": ("sbuf", [128, 3 * K], "int32"),
+    "ho": ("sbuf", [128, 3 * K], "uint16"),
+    "wa": ("sbuf", [128, 3 * K], "int32"),
+    "wb": ("sbuf", [128, 3 * K], "int32"),
+    "wc": ("sbuf", [128, 3 * K], "int32"),
+    "wo": ("sbuf", [128, 3 * K], "uint16"),
+    "land0": ("sbuf", [128, K], "float32"),
 }
 for _t in (1, 2, 3):
-    SCRATCH["bs%d" % _t] = ("sbuf", [128, K], "float32")
-    SCRATCH["bl%d" % _t] = ("sbuf", [128, K], "float32")
-for _n in ("pv", "pw", "pu", "pxa", "pxb", "pe1", "pe2", "pw2"):
+    SCRATCH["land%d" % _t] = ("sbuf", [128, K], "float32")
+    SCRATCH["sm%d" % _t] = ("sbuf", [128, 2 * NP], "bfloat16")
+    SCRATCH["hp%d" % _t] = ("sbuf", [128, 2 * K], "float32")
+for _n in ("pv", "pw", "px0", "px1", "pu", "pe", "pf1", "pf2"):
     SCRATCH[_n] = ("psum", [128, 512], "float32")
 
-SEMAPHORES = ["cv", "ca", "cp", "cg", "dr", "dr2", "dh", "dt0", "dt1", "dt2", "dy",
+SEMAPHORES = ["cv", "ca", "cp", "cg", "dr0", "dr1", "dr2", "dh", "dt0", "dt1", "dt2", "dt3", "dy",
               "ar0", "ar1", "ar2", "ar3", "sn0", "sn1", "sn2", "sn3"]
 
 
@@ -60,12 +66,28 @@ def nbits(m):
     return bin(m).count("1")
 
 
+def hop_mask(src, dst, topo):
+    return topo.mask(src, dst)
+
+
+def span(start, count, step):
+    return slice(start, start + (count - 1) * step + 1, step)
+
+
+def pieces(level):
+    s = level % PB
+    lo, hi = max(((0, s), (s, PB)), key=lambda r: r[1] - r[0])
+    c = 1 << (hi - lo)
+    return [(j, 1 << lo, (j >> s) | ((j << (PB - s)) & (NP - 1)), 1 << ((lo - s) % PB), c)
+            for j in range(NP) if (j >> lo) & (c - 1) == 0]
+
+
 def rank_program(g, core, T, topo):
     cores = list(T.cores)
     n = len(cores)
     rank = T.rank_of(core)
     sem = T.sem
-    land = [T.e1l, T.bl1, T.bl2, T.bl3]
+    land = [T["land%d" % k] for k in range(4)]
 
     if rank is None:
         for r in range(n - 1):
@@ -73,7 +95,7 @@ def rank_program(g, core, T, topo):
                 continue
             dst = cores[r + 1]
             rid, pid = topo.addr(dst, core)
-            m_in, m_out = topo.mask(cores[r], core), topo.mask(core, dst)
+            m_in, m_out = hop_mask(cores[r], core, topo), hop_mask(core, dst, topo)
             for k in range(4):
                 g.wait_ge(sem["ar%d" % k], nbits(m_in))
                 g.remote_dma(land[k][:], land[k][:], sem["ar%d" % k], sem["sn%d" % k], pid, rid, m_out)
@@ -99,237 +121,290 @@ def rank_program(g, core, T, topo):
 
     V, S_, P = g.vector, g.scalar, g.tensor
 
+    def vop(inst_fn, *evs):
+        need("v", *evs)
+        return done("v", inst_fn())
+
     if not last:
         nxt = relay_for(core, cores[rank + 1], T, topo)
         nxt = cores[rank + 1] if nxt is None else nxt
         rid, pid = topo.addr(nxt, core)
-        m_out = topo.mask(core, nxt)
+        m_out = hop_mask(core, nxt, topo)
     if not first:
         prv = relay_for(cores[rank - 1], core, T, topo)
         prv = cores[rank - 1] if prv is None else prv
-        n_in = nbits(topo.mask(prv, core))
+        n_in = nbits(hop_mask(prv, core, topo))
 
-    def send(k, src):
-        g.remote_dma(land[k][:], src, sem["ar%d" % k], sem["sn%d" % k], pid, rid, m_out)
-
-    lo = [128 * c0 for c0, c1 in CH]
-    hi = lo[1:] + [W]
-    nr = 2 * S if first else M * S
-    g.sync.dma_start(T.rs[:, 0:nr], T.res[:, 0:nr]).then_inc(sem.dr, 16)
+    g.sync.dma_start(T.rs[:, 0:S], T.res[:, 0:S]).then_inc(sem.dr0, 16)
     S_.dma_start(T.hws[:], T.hw[:]).then_inc(sem.dh, 16)
-    S_.dma_start(T.tabw[:, lo[0]:hi[0]], T.tab[:, lo[0]:hi[0]]).then_inc(sem.dt0, 16)
-    g.sync.dma_start(T.tabw[:, lo[1]:hi[1]], T.tab[:, lo[1]:hi[1]]).then_inc(sem.dt1, 16)
-    S_.dma_start(T.tabw[:, lo[2]:hi[2]], T.tab[:, lo[2]:hi[2]]).then_inc(sem.dt2, 16)
-    DR, DH = ("dr", 16), ("dh", 16)
-    DR2 = DR
+    S_.dma_start(T.rs[:, S:2 * S + 32], T.res[:, S:2 * S + 32]).then_inc(sem.dr1, 16)
+    if not first:
+        S_.dma_start(T.rs[:, 2 * S + 32:M * S], T.res[:, 2 * S + 32:M * S]).then_inc(sem.dr2, 16)
+    for i, (c0, c1) in enumerate(CH):
+        g.sync.dma_start(T.tabw[:, 128 * c0:128 * c1], T.tab[:, 128 * c0:128 * c1]).then_inc(sem["dt%d" % i], 16)
     if first:
-        need("s", ("dt1", 16))
-        g.sync.dma_start(T.rs[:, nr:M * S], T.res[:, nr:M * S]).then_inc(sem.dr2, 16)
-        DR2 = ("dr2", 16)
+        g.sync.dma_start(T.rs[:, 2 * S + 32:M * S], T.res[:, 2 * S + 32:M * S]).then_inc(sem.dr2, 16)
+    DR0, DR1, DR2, DH = ("dr0", 16), ("dr1", 16), ("dr2", 16), ("dh", 16)
+    DT = ("dt%d" % (len(CH) - 1), 16)
 
     m_gm = done("v", V.memset(T.gm[:], 1.0))
     m_z = done("v", V.memset(T.z[:], 0.0))
-    done("v", V.memset(T.idn[:], 1.0))
-    m_id = done("v", V.memset(T.nidn[:], -256.0))
-    i_p = done("g", g.iota(T.p8[:], [[0, 1]], 0, 8))
+    done("v", V.memset(T.zero[:], 0.0))
+    m_pad = done("v", V.memset(T.rs[:, M * S:(M - 1) * S + NP], 0.0))
+    done("v", V.memset(T.idn[:], 256.0))
+    m_id = done("v", V.memset(T.nidn[:], -1.0))
+    i_p = done("g", g.iota(T.pi[:, 0:1], [[0, 1]], 0, 1))
     need("g", m_gm)
     s1 = done("g", g.affine_select(T.gm[:], T.gm[:], [[-16, 8]], A.is_ge, 0.0, 0, 1))
-    for c0, c1 in CH:
+    for c0, c1 in CH[:-1]:
         done("g", g.iota(T.cb[:, c0:c1], [[128, c1 - c0]], 0, 0))
-    done("g", g.iota(T.cb[:, K:32], [[0, 32 - K]], 0, 0))
-    i_cb = done("g", g.iota(T.cb[:, 32:64], [[128, 32]], 0, 0))
     need("g", s1)
     s_gm = done("g", g.affine_select(T.gm[:], T.gm[:], [[16, 8]], A.is_ge, 0.0, 15, -1))
+    i_cb = done("g", g.iota(T.cb[:, K:2 * K], [[16, K]], 0, 0))
     need("g", m_id)
-    done("g", g.affine_select(T.idn[:], T.idn[:], [[-1, 128]], A.is_equal, 0.0, 0, 1))
-    s_id = done("g", g.affine_select(T.nidn[:], T.nidn[:], [[-1, 128]], A.is_equal, 0.0, 0, 1))
-    need("v", i_p)
-    k1 = done("v", V.tensor_scalar(T.p8b[:], T.p8[:], 127, None, A.bitwise_and))
-    need("v", k1)
-    k2 = done("v", V.tensor_copy(T.a8[:], T.p8b[:]))
-    need("v", k2, i_cb)
-    k_base = done("v", V.tensor_scalar(T.base[:], T.cb[:], T.a8[:], None, A.add))
-    ZU, ZV, ZWW = 0, ZW, 2 * ZW
+    for t_id in (T.nidn, T.idn):
+        s_id = done("g", g.affine_select(t_id[:], t_id[:], [[-1, 128]], A.is_equal, 0.0, 0, 1))
+
+    A1, A8 = T.pf[:, 0:1], T.pf[:, 1:2]
+    e = vop(lambda: V.tensor_scalar(T.pi[:, 1:2], T.pi[:, 0:1], 15, None, A.bitwise_and), i_p)
+    vop(lambda: V.tensor_copy(A1, T.pi[:, 1:2]), e)
+    e8 = vop(lambda: V.tensor_scalar(A8, T.pi[:, 1:2], 8.0, None, A.mult))
+    k_base0 = vop(lambda: V.tensor_scalar(T.base[:, 0:K0], T.cb[:, 0:K0], A8, None, A.add), e8, i_cb)
+    kev = {}
+
+    def orders():
+        nu = [T.nu[:, 4 * K * i:4 * K * (i + 1)] for i in range(6)]
+        for i, t in enumerate((1, 2, 3, 0)):
+            e = vop(lambda: V.tensor_scalar(T.nu[:, K * i:K * (i + 1)], T.cb[:, K:2 * K], A1,
+                                            float(1 << (PB - (rank + t) % PB)), A.add, A.mult))
+        yield
+        vop(lambda: V.tensor_scalar(nu[1], nu[0], NP - 1, None, A.bitwise_and), e)
+        e = vop(lambda: V.tensor_scalar(nu[2], nu[0], PB, None, A.logical_shift_right))
+        yield
+        e = vop(lambda: V.tensor_tensor(nu[3], nu[1], nu[2], A.add), e)
+        yield
+        kev["list"] = vop(lambda: V.tensor_copy(T.pl[:], nu[3]), e)
+        vop(lambda: V.tensor_scalar(nu[4], nu[3], 8.0, None, A.mult))
+        e = vop(lambda: V.tensor_scalar(nu[5], nu[3], float(S), 256.0, A.is_ge, A.mult))
+        yield
+        kev["base"] = vop(lambda: V.tensor_tensor(T.base[:, K:3 * K], T.nu[:, 16 * K:18 * K], T.nu[:, 20 * K:22 * K],
+                                                  A.add), e)
+
+    side = orders()
+    next(side)
+    if not first:
+        for _ in side:
+            pass
+
+    zev = {}
     need("v", m_z, s_gm, DH)
-    z_w = done("v", V.tensor_scalar(T.z[:, ZWW + 15:ZWW + 143:16], T.gm[:], T.hws[:, 2:3], -256.0, A.mult, A.mult))
-    z_u = done("v", V.tensor_scalar(T.z[:, ZU + 15:ZU + 143:16], T.gm[:], T.hws[:, 0:1], None, A.mult))
-    z_v = done("v", V.tensor_scalar(T.z[:, ZV + 15:ZV + 143:16], T.gm[:], T.hws[:, 1:2], -256.0, A.mult, A.mult))
+    for i, (name, (col, scale)) in enumerate(TILES.items()):
+        if not (last and col == 1):
+            zev[name] = done("v", V.tensor_scalar(T.z[:, span(i * ZW + C0, 8, 16)], T.gm[:], T.hws[:, col:col + 1],
+                                                  scale, A.mult, A.mult))
+    next(side, None)
 
-    def hash16(out, zo, buf, c0, cols):
-        for a in range(16):
-            inst = P.matmul(out[:, 0:cols // 16], T.z[:, zo + 15 - a:zo + 143 - a],
-                            buf[:, c0 + a:c0 + cols:16], a == 0, a == 15)
-        return done("p", inst)
+    def tile(name, row):
+        c = list(TILES).index(name) * ZW + C0 - row
+        return T.z[:, c:c + 128]
 
-    def xbanks(t):
+    def hash_rows(out, name, buf, c0, cols, start, stop, rows=range(16)):
+        need("p", zev[name])
+        for a in rows:
+            inst = P.matmul(out[:, 0:cols], tile(name, a), buf[:, span(c0 + a, cols, 16)],
+                            start and a == rows[0], stop and a == rows[-1])
+        return done("p", inst) if stop else None
+
+    def xparts(t):
         if last and t == M - 1:
-            return [(T.pxa, 0, S // 2), (T.pxb, S // 2, S)]
-        return [(T.pxa, 0, S)]
+            return [(16 * c0, 16 * c1, b) for (c0, c1), b in zip(FIN, (T.pe, T.pf1, T.pf2))]
+        return [(0, H, T.px0), (H, NP, T.px1)]
 
-    def xpre(t):
-        for bank, c0, c1 in xbanks(t):
-            P.matmul(bank[:, 0:c1 - c0], T.idn[:], T.rs[:, t * S + c0:t * S + c1], True, False)
+    def pre(t):
+        need("p", thr[t], s_id)
+        if t > 1 and not last:
+            P.matmul(T.pv[:, 0:2 * K], tile("w", 0), T.zero[:], True, False)
+            hash_rows(T.pv, "vn", T.thr, (t - 1) * NP, K, False, False)
+        if t < M - 1:
+            hash_rows(T.pw, "wn", T.thr, (t - 1) * NP, K, True, False)
+        for x0, x1, b in xparts(t):
+            P.matmul(b[:, 0:x1 - x0], T.nidn[:], T.thr[:, (t - 1) * NP + x0:(t - 1) * NP + x1], True, False)
 
-    def wlist(t, src_ev, boff):
-        o = 32 * t
-        src = T.wi[:, 0:K] if t == 0 else T.wa[:, o:o + K]
-        need("v", src_ev)
-        e = done("v", V.tensor_scalar(T.wb[:, o:o + K], src, 7, None, A.bitwise_and))
-        need("v", e, k_base)
-        e = done("v", V.tensor_tensor(T.wc[:, o:o + K], T.wb[:, o:o + K], T.base[:, boff:boff + K], A.add))
-        need("v", e)
-        return done("v", V.tensor_copy(T.wo[:, o:o + K], T.wc[:, o:o + K]))
+    def order(t):
+        i = (t - 1) % M
+        return T.pl[:, K * i:K * (i + 1)]
+
+    def permute(out, o0, i0, level, bias, scale):
+        if len(pieces(level)) > 4:
+            need("a", kev["list"], DR2, m_pad)
+            return done("a", S_.activation(out[:, o0:o0 + NP], T.rs[:, i0:i0 + NP].indirect(order(level - rank)),
+                                           F.Identity, bias, scale))
+        for j, sj, s, ss, c in pieces(level):
+            inst = S_.activation(out[:, span(o0 + j, c, sj)], T.rs[:, span(i0 + s, c, ss)], F.Identity, bias, scale)
+        return done("a", inst)
+
+    def make_thr(t):
+        need("a", DR1, *([DR2, m_pad] if t > 1 else []))
+        level = 0 if last and t == M - 1 else rank + t
+        return permute(T.thr, (t - 1) * NP, t * S, level, 256.0, -1.0)
+
+    def wlist(t, bank, ev, cols):
+        o = K * t
+        e0 = vop(lambda: V.tensor_copy(T.wa[:, o:o + cols], bank[:, 0:cols]), ev)
+        next(side, None)
+        e = vop(lambda: V.tensor_scalar(T.wb[:, o:o + cols], T.wa[:, o:o + cols], 7, None, A.bitwise_and), e0)
+        next(side, None)
+        e = vop(lambda: V.tensor_tensor(T.wc[:, o:o + cols], T.wb[:, o:o + cols], T.base[:, o:o + cols], A.add), e)
+        next(side, None)
+        return e0, vop(lambda: V.tensor_copy(T.wo[:, o:o + cols], T.wc[:, o:o + cols]), e)
 
     def hlist(t, ev):
-        o = 32 * (t - 1)
-        need("v", ev)
-        e = done("v", V.tensor_scalar(T.hb[:, o:o + K], T.ha[:, o:o + K], W - 1, None, A.bitwise_and))
-        need("v", e)
-        return done("v", V.tensor_copy(T.ho[:, o:o + K], T.hb[:, o:o + K]))
-
-    R256 = -1.0 / 256.0
-
-    nw = 2 if first else 3
-    need("p", z_w, DR)
-    p_w = hash16(T.pw, ZWW, T.rs, 0, nw * S)
-    need("p", z_u)
-    p_u = hash16(T.pu, ZU, T.rs, 0, S)
-    ev_e23 = None
-    if not last:
-        need("p", z_v)
-        p_e = hash16(T.pe1, ZV, T.rs, S, S if first else 3 * S)
-    need("p", s_id)
-    xpre(1)
-
-    need("a", DR)
-    nt = 1 if first else 3
-    ev_thr = {1: done("a", S_.activation(T.thr[:, 0:nt * S], T.rs[:, S:(1 + nt) * S], F.Identity, 256.0, -1.0))}
-    if not first:
-        ev_thr[2] = ev_thr[3] = ev_thr[1]
-    if not last:
-        need("a", p_e)
-        a_e1 = done("a", S_.activation(T.e1s[:], T.pe1[:, 0:K], F.Identity, 0.0, R256))
-        if not first:
-            ev_e23 = done("a", S_.activation(T.e23[:], T.pe1[:, K:3 * K], F.Identity, 0.0, R256))
-        need("g", a_e1)
-        send(0, T.e1s[:])
-
-    need("v", p_w)
-    w0 = done("v", V.tensor_scalar(T.wi[:, 0:nw * K], T.pw[:, 0:nw * K], R256, None, A.mult))
-    wl = wlist(0, w0, 0)
-    if first:
-        need("v", p_u)
-        hl = hlist(1, done("v", V.tensor_copy(T.ha[:, 0:K], T.pu[:, 0:K])))
-    for i, (c0, c1) in enumerate(CH):
-        need("v", wl, ("dt%d" % i, 16))
-        sc = done("v", V.tensor_copy(T.tabw[:, lo[i]:hi[i]].indirect(T.wo[:, c0:c1]), T.rs[:, 16 * c0:16 * c1]))
-    if not first:
-        need("v", p_u, ("ar0", n_in))
-        ev_ue = done("v", V.tensor_tensor(T.ue[:], T.pu[:, 0:K], T.e1l[:], A.add))
-    we = {1: (T.wi[:, K:2 * K], w0), 2: (T.wi[:, 2 * K:3 * K], w0)}
+        o = K * (t - 1)
+        e = vop(lambda: V.tensor_scalar(T.hb[:, o:o + K], T.ha[:, o:o + K], W - 1, None, A.bitwise_and), ev)
+        return vop(lambda: V.tensor_copy(T.ho[:, o:o + K], T.hb[:, o:o + K]), e)
 
     ny = [0]
 
-    def store(q, out, src):
-        Q[q].dma_start(out, src).then_inc(sem.dy, 16)
+    def store(q, t, c0, c1):
+        natural = (rank + t) % PB == 0 or (last and t == M - 1)
+        src = T.rs[:, c0:c1] if t == 0 else (T.xs if natural else T.yb)[:, (t - 1) * NP + c0:(t - 1) * NP + c1]
+        Q[q].dma_start(T.y[:, t * S + c0:t * S + c1], src).then_inc(sem.dy, 16)
         ny[0] += 16
 
-    if last:
-        need("s", DR)
-        store("s", T.y[:, 0:S], T.rs[:, 0:S])
+    def unpermute(q, t):
+        tb = (t - 1) * NP
+        if (rank + t) % PB == 0:
+            return ev_x[t]
+        need(q, ev_x[t])
+        if len(pieces(rank + t)) > 8:
+            return vop(lambda: V.tensor_copy(T.yb[:, tb:tb + NP].indirect(order(t)), T.xs[:, tb:tb + NP]))
+        for j, sj, s, ss, c in pieces(rank + t):
+            out, src = T.yb[:, span(tb + s, c, ss)], T.xs[:, span(tb + j, c, sj)]
+            inst = V.tensor_copy(out, src) if q == "v" else S_.activation(out, src, F.Identity)
+        return done(q, inst)
+
+    need("p", DR0)
+    p_w = hash_rows(T.pf1, "w", T.rs, 0, K0, True, True)
+    thr = {1: make_thr(1)}
+    if not first:
+        need("a", DR0)
+        a_e0 = permute(T.e0p, 0, 0, rank, 0.0, 1.0)
+    if first:
+        need("p", DR1)
+        p_u = hash_rows(T.pu, "u", T.rs, 0, K, True, True)
+    need("p", thr[1])
+    if not last:
+        p_e = hash_rows(T.pe, "vn", T.thr, 0, K, True, True)
+        need("a", p_e)
+        a_e1 = done("a", S_.activation(T.e1s[:], T.pe[:, 0:K], F.Identity))
+        need("g", a_e1)
+        g.remote_dma(land[0][:], T.e1s[:], sem.ar0, sem.sn0, pid, rid, m_out)
+    if not first:
+        need("p", a_e0)
+        p_u = hash_rows(T.pu, "u", T.e0p, 0, K, True, True)
+    pre(1)
+    if not first:
+        for t in (2, 3):
+            thr[t] = make_thr(t)
+
+    v_w, wl = wlist(0, T.pf1, p_w, K0)
+    for i, (c0, c1) in enumerate(CH[:-1]):
+        sc = vop(lambda: V.tensor_copy(T.tabw[:, 128 * c0:128 * c1].indirect(T.wo[:, c0:c1]),
+                                       T.rs[:, 16 * c0:16 * c1]), wl, ("dt%d" % i, 16))
+        if first and i == 0:
+            hl = hlist(1, vop(lambda: V.tensor_copy(T.ha[:, 0:K], T.pu[:, 0:K]), p_u))
+    if not first:
+        ev_ue = vop(lambda: V.tensor_tensor(T.ue[:], T.pu[:, 0:K], land[0][:], A.add), p_u, ("ar0", n_in))
+        need("s", DR0, DR2)
+        store("s", 0, 0, S)
+
+    table = T.tabw[:, 0:W]
+    ev_x = {}
 
     for t in range(1, M):
-        o = 32 * (t - 1)
-        sm = T["sm%d" % t]
-        xt = T.xs[:, (t - 1) * S:t * S]
+        o = K * (t - 1)
+        sm, hp = T["sm%d" % t], T["hp%d" % t]
+        tb = (t - 1) * NP
         if first:
             if t > 1:
-                need("v", p_u)
-                hl = hlist(t, done("v", V.tensor_copy(T.ha[:, o:o + K], T.pu[:, 0:K])))
+                hl = hlist(t, vop(lambda: V.tensor_copy(T.ha[:, o:o + K], T.pu[:, 0:K]), p_u))
+        elif t == 1:
+            hl = hlist(t, vop(lambda: V.tensor_tensor(T.ha[:, o:o + K], T.ue[:], land[t][:], A.add),
+                              ev_ue, ("ar1", n_in)))
         else:
-            if t == 1:
-                need("v", ev_ue, ("ar1", n_in))
-                e = V.tensor_tensor(T.ha[:, o:o + K], T.ue[:], T.bl1[:], A.add)
-            else:
-                need("v", p_u, ("ar%d" % t, n_in))
-                e = V.tensor_tensor(T.ha[:, o:o + K], T.pu[:, 0:K], land[t][:], A.add)
-            hl = hlist(t, done("v", e))
-        offs = T.ho[:, o:o + K]
-        need("v", hl, sc, ev_thr[t])
-        g_c = done("v", V.tensor_tensor(sm[:, S:2 * S], T.tabw[:, 0:W].indirect(offs),
-                                        T.thr[:, (t - 1) * S:t * S], A.is_ge))
-        need("a", hl, sc)
-        g_s = done("a", S_.activation(sm[:, 0:S], T.tabw[:, 0:W].indirect(offs), F.Identity, 0.0, R256))
+            hl = hlist(t, vop(lambda: V.tensor_tensor(T.ha[:, o:o + K], T.pu[:, 0:K], land[t][:], A.add),
+                              p_u, ("ar%d" % t, n_in)))
 
-        need("p", g_c, g_s)
-        if not last:
-            p_v = hash16(T.pv, ZV, sm, 0, 2 * S)
-        if t < M - 1:
-            p_w = hash16(T.pw, ZWW, sm, 0, S)
-        p_x = []
-        for bank, c0, c1 in xbanks(t):
-            P.matmul(bank[:, 0:c1 - c0], T.nidn[:], sm[:, c0:c1], False, False)
-            p_x.append(done("p", P.matmul(bank[:, 0:c1 - c0], T.nidn[:], sm[:, S + c0:S + c1], False, True)))
+        def gather(places, offs):
+            c0, count, step = places
+            g_c = vop(lambda: V.tensor_tensor(sm[:, span(NP + c0, count, step)], table.indirect(offs),
+                                              T.thr[:, span(tb + c0, count, step)], A.is_lt), hl, sc, thr[t], DT)
+            need("a", hl, sc, DT)
+            g_s = done("a", S_.activation(sm[:, span(c0, count, step)], table.indirect(offs), F.Identity,
+                                          0.0, 1.0 / 256.0))
+            return g_c, g_s
 
-        if not last:
-            need("v", p_v)
-            if t == 1:
-                e = V.tensor_copy(T.vt[:, o:o + K], T.pv[:, K:2 * K])
-            else:
-                need("v", ev_e23)
-                e = V.tensor_tensor(T.vt[:, o:o + K], T.pv[:, K:2 * K], T.e23[:, (t - 2) * K:(t - 1) * K], A.add)
-            need("v", done("v", e))
-            e = done("v", V.tensor_tensor(T["bs%d" % t][:], T.pv[:, 0:K], T.vt[:, o:o + K], A.add))
-            need("g", e)
-            send(t, T["bs%d" % t][:])
+        def xsum(x0, x1, b):
+            P.matmul(b[:, 0:x1 - x0], T.idn[:], sm[:, x0:x1], False, False)
+            return done("p", P.matmul(b[:, 0:x1 - x0], T.idn[:], sm[:, NP + x0:NP + x1], False, True))
 
         if last and t == M - 1:
-            h = S // 2
-            need("a", p_x[0])
-            ea = done("a", S_.activation(T.xs[:, 2 * S:2 * S + h], T.pxa[:, 0:h], F.Identity))
-            need("v", p_x[1])
-            eb = done("v", V.tensor_copy(T.xs[:, 2 * S + h:3 * S], T.pxb[:, 0:h]))
-            need("a", ea)
-            store("a", T.y[:, t * S:t * S + h], T.xs[:, 2 * S:2 * S + h])
-            need("s", eb)
-            store("s", T.y[:, t * S + h:M * S], T.xs[:, 2 * S + h:3 * S])
+            p_x = []
+            for x0, x1, b in xparts(t):
+                need("p", *gather((x0, x1 - x0, 1), T.ho[:, o + x0 // 16:o + x1 // 16]))
+                p_x.append(xsum(x0, x1, b))
+            for i, (x0, x1, b) in enumerate(xparts(t)):
+                if i == 1:
+                    need("a", p_x[i])
+                    e = done("a", S_.activation(T.xs[:, tb + x0:tb + x1], b[:, 0:x1 - x0], F.Identity))
+                    need("a", e)
+                    store("a", t, x0, x1)
+                else:
+                    e = vop(lambda: V.tensor_copy(T.xs[:, tb + x0:tb + x1], b[:, 0:x1 - x0]), p_x[i])
+                    need("s", e)
+                    store("s", t, x0, x1)
             break
 
-        need("a", p_x[0])
-        ev_x = done("a", S_.activation(xt, T.pxa[:, 0:S], F.Identity))
+        for b in range(2):
+            need("p", *gather((b, H, 2), T.ho[:, o + 16 * b:o + 16 * b + 16]))
+            if not last:
+                p_v = hash_rows(T.pv, "v256", sm, 0, 2 * K, t == 1 and b == 0, b == 1, range(b, 16, 2))
+            if t < M - 1:
+                p_w = hash_rows(T.pw, "w256", sm, 0, K, False, b == 1, range(b, 16, 2))
         if not last:
-            need("s", ("sn%d" % t, nbits(m_out)))
-            if t == 1:
-                need("s", DR)
-                store("s", T.y[:, 0:S], T.rs[:, 0:S])
-        need("s", ev_x)
-        store("s", T.y[:, t * S:(t + 1) * S], xt)
+            v_h = vop(lambda: V.tensor_copy(hp[:], T.pv[:, 0:2 * K]), p_v)
+            need("g", v_h)
+            g.remote_dma_fused([RemoteDMATransfer(
+                dst_ids=[DstId(rid=rid, pnc=pid)], dma_engine_mask=m_out, remote_sem=sem["ar%d" % t],
+                srcs=[hp[:, 0:K], hp[:, K:2 * K]], dsts=[land[t][:]], alu_op=1)],
+                local_sem=sem["sn%d" % t])
+        a_x = []
+        for x0, x1, b in xparts(t):
+            need("a", xsum(x0, x1, b))
+            a_x.append(done("a", S_.activation(T.xs[:, tb + x0:tb + x1], b[:, 0:x1 - x0], F.Identity)))
+        ev_x[t] = a_x[-1]
+
         if t == M - 1:
+            need("s", ("sn3", nbits(m_out)))
+            if first:
+                store("s", 0, 0, S)
+            for u in range(1, M):
+                need("s", unpermute("v", u))
+                store("s", u, 0, S)
             break
 
-        need("p", ev_x)
-        p_u = hash16(T.pu, ZU, T.xs, (t - 1) * S, S)
+        v_w, wl = wlist(t, T.pw, p_w, K)
+        sc = vop(lambda: V.tensor_copy(T.tabw[:].indirect(T.wo[:, K * t:K * (t + 1)]), T.xs[:, tb:tb + NP]),
+                 wl, ev_x[t])
+        need("p", ev_x[t])
+        p_u = hash_rows(T.pu, "u", T.xs, tb, K, True, True)
         if first:
-            need("p", DR2)
-            if t == 1:
-                p_e2 = hash16(T.pe2, ZV, T.rs, 2 * S, 2 * S)
-                p_w2 = hash16(T.pw2, ZWW, T.rs, 2 * S, S)
-        xpre(t + 1)
-        if first:
-            need("a", DR2)
-            ev_thr[t + 1] = done("a", S_.activation(T.thr[:, t * S:(t + 1) * S], T.rs[:, (t + 1) * S:(t + 2) * S],
-                                                    F.Identity, 256.0, -1.0))
-            if t == 1:
-                need("a", p_e2)
-                ev_e23 = done("a", S_.activation(T.e23[:], T.pe2[:, 0:2 * K], F.Identity, 0.0, R256))
-                need("a", p_w2)
-                we[2] = (T.we2[:], done("a", S_.activation(T.we2[:], T.pw2[:, 0:K], F.Identity, 0.0, R256)))
-
-        need("v", p_w, we[t][1])
-        e = done("v", V.tensor_tensor(T.wa[:, 32 * t:32 * t + K], T.pw[:, 0:K], we[t][0], A.add))
-        wl = wlist(t, e, 32)
-        need("v", wl, ev_x)
-        sc = done("v", V.tensor_copy(T.tabw[:, 0:W].indirect(T.wo[:, 32 * t:32 * t + K]), xt))
+            thr[t + 1] = make_thr(t + 1)
+        need("p", v_w)
+        pre(t + 1)
+        if last:
+            need("s", unpermute("a", t))
+            store("s", t, 0, S)
 
     need("s", ("dy", ny[0]))
     for q in ("v", "a", "p", "g"):

@@ -7,8 +7,11 @@ NP = 1 << PB
 K = NP // 16
 K0 = S // 16
 H = NP // 2
+NB = 2
+NC = 1 << NB
 ZW, C0 = 144, 15
-CH = [(0, 16), (16, 26), (26, 30), (30, 32)]
+SC = [(0, 8), (8, 16), (16, 24), (24, 30)]
+CH = [(0, 8), (8, 16), (16, 24), (24, 32)]
 FIN = [(0, 12), (12, 22), (22, 30)]
 TILES = {"w": (2, 1.0), "vn": (1, -1.0), "u": (0, 1.0), "wn": (2, -1.0),
          "v256": (1, 256.0), "w256": (2, 256.0)}
@@ -18,7 +21,6 @@ SCRATCH = {
     "rs": ("sbuf", [128, (M - 1) * S + NP], "bfloat16"),
     "hws": ("sbuf", [128, 3], "bfloat16"),
     "z": ("sbuf", [128, len(TILES) * ZW], "bfloat16"),
-    "zero": ("sbuf", [128, 2 * K], "bfloat16"),
     "gm": ("sbuf", [128, 8], "bfloat16"),
     "idn": ("sbuf", [128, 128], "bfloat16"),
     "nidn": ("sbuf", [128, 128], "bfloat16"),
@@ -75,7 +77,7 @@ def span(start, count, step):
 
 
 def pieces(level):
-    s = level % PB
+    s = NB * level % PB
     lo, hi = max(((0, s), (s, PB)), key=lambda r: r[1] - r[0])
     c = 1 << (hi - lo)
     return [(j, 1 << lo, (j >> s) | ((j << (PB - s)) & (NP - 1)), 1 << ((lo - s) % PB), c)
@@ -137,11 +139,13 @@ def rank_program(g, core, T, topo):
 
     g.sync.dma_start(T.rs[:, 0:S], T.res[:, 0:S]).then_inc(sem.dr0, 16)
     S_.dma_start(T.hws[:], T.hw[:]).then_inc(sem.dh, 16)
-    S_.dma_start(T.rs[:, S:2 * S + 32], T.res[:, S:2 * S + 32]).then_inc(sem.dr1, 16)
     if not first:
+        S_.dma_start(T.rs[:, S:2 * S + 32], T.res[:, S:2 * S + 32]).then_inc(sem.dr1, 16)
         S_.dma_start(T.rs[:, 2 * S + 32:M * S], T.res[:, 2 * S + 32:M * S]).then_inc(sem.dr2, 16)
     for i, (c0, c1) in enumerate(CH):
         g.sync.dma_start(T.tabw[:, 128 * c0:128 * c1], T.tab[:, 128 * c0:128 * c1]).then_inc(sem["dt%d" % i], 16)
+        if first and i == 0:
+            g.sync.dma_start(T.rs[:, S:2 * S + 32], T.res[:, S:2 * S + 32]).then_inc(sem.dr1, 16)
     if first:
         g.sync.dma_start(T.rs[:, 2 * S + 32:M * S], T.res[:, 2 * S + 32:M * S]).then_inc(sem.dr2, 16)
     DR0, DR1, DR2, DH = ("dr0", 16), ("dr1", 16), ("dr2", 16), ("dh", 16)
@@ -149,15 +153,13 @@ def rank_program(g, core, T, topo):
 
     m_gm = done("v", V.memset(T.gm[:], 1.0))
     m_z = done("v", V.memset(T.z[:], 0.0))
-    done("v", V.memset(T.zero[:], 0.0))
     m_pad = done("v", V.memset(T.rs[:, M * S:(M - 1) * S + NP], 0.0))
     done("v", V.memset(T.idn[:], 256.0))
     m_id = done("v", V.memset(T.nidn[:], -1.0))
     i_p = done("g", g.iota(T.pi[:, 0:1], [[0, 1]], 0, 1))
     need("g", m_gm)
     s1 = done("g", g.affine_select(T.gm[:], T.gm[:], [[-16, 8]], A.is_ge, 0.0, 0, 1))
-    for c0, c1 in CH[:-1]:
-        done("g", g.iota(T.cb[:, c0:c1], [[128, c1 - c0]], 0, 0))
+    done("g", g.iota(T.cb[:, 0:K], [[0, 4], [128, 8]], 0, 0))
     need("g", s1)
     s_gm = done("g", g.affine_select(T.gm[:], T.gm[:], [[16, 8]], A.is_ge, 0.0, 15, -1))
     i_cb = done("g", g.iota(T.cb[:, K:2 * K], [[16, K]], 0, 0))
@@ -176,7 +178,7 @@ def rank_program(g, core, T, topo):
         nu = [T.nu[:, 4 * K * i:4 * K * (i + 1)] for i in range(6)]
         for i, t in enumerate((1, 2, 3, 0)):
             e = vop(lambda: V.tensor_scalar(T.nu[:, K * i:K * (i + 1)], T.cb[:, K:2 * K], A1,
-                                            float(1 << (PB - (rank + t) % PB)), A.add, A.mult))
+                                            float(1 << (PB - NB * (rank + t) % PB)), A.add, A.mult))
         yield
         vop(lambda: V.tensor_scalar(nu[1], nu[0], NP - 1, None, A.bitwise_and), e)
         e = vop(lambda: V.tensor_scalar(nu[2], nu[0], PB, None, A.logical_shift_right))
@@ -191,17 +193,22 @@ def rank_program(g, core, T, topo):
                                                   A.add), e)
 
     side = orders()
-    next(side)
     if not first:
         for _ in side:
             pass
 
     zev = {}
-    need("v", m_z, s_gm, DH)
-    for i, (name, (col, scale)) in enumerate(TILES.items()):
-        if not (last and col == 1):
-            zev[name] = done("v", V.tensor_scalar(T.z[:, span(i * ZW + C0, 8, 16)], T.gm[:], T.hws[:, col:col + 1],
-                                                  scale, A.mult, A.mult))
+
+    def fill(names):
+        for name in names:
+            col, scale = TILES[name]
+            if not (last and col == 1):
+                c = list(TILES).index(name) * ZW + C0
+                zev[name] = vop(lambda: V.tensor_scalar(T.z[:, span(c, 8, 16)], T.gm[:], T.hws[:, col:col + 1],
+                                                        scale, A.mult, A.mult), m_z, s_gm, DH)
+
+    fill(list(TILES))
+    next(side, None)
     next(side, None)
 
     def tile(name, row):
@@ -223,8 +230,7 @@ def rank_program(g, core, T, topo):
     def pre(t):
         need("p", thr[t], s_id)
         if t > 1 and not last:
-            P.matmul(T.pv[:, 0:2 * K], tile("w", 0), T.zero[:], True, False)
-            hash_rows(T.pv, "vn", T.thr, (t - 1) * NP, K, False, False)
+            hash_rows(T.pv, "vn", T.thr, (t - 1) * NP, K, True, False)
         if t < M - 1:
             hash_rows(T.pw, "wn", T.thr, (t - 1) * NP, K, True, False)
         for x0, x1, b in xparts(t):
@@ -308,11 +314,15 @@ def rank_program(g, core, T, topo):
             thr[t] = make_thr(t)
 
     v_w, wl = wlist(0, T.pf1, p_w, K0)
-    for i, (c0, c1) in enumerate(CH[:-1]):
+    for i, (c0, c1) in enumerate(SC):
         sc = vop(lambda: V.tensor_copy(T.tabw[:, 128 * c0:128 * c1].indirect(T.wo[:, c0:c1]),
                                        T.rs[:, 16 * c0:16 * c1]), wl, ("dt%d" % i, 16))
-        if first and i == 0:
-            hl = hlist(1, vop(lambda: V.tensor_copy(T.ha[:, 0:K], T.pu[:, 0:K]), p_u))
+        if first and i < 3:
+            hl = [lambda: vop(lambda: V.tensor_copy(T.ha[:, 0:K], T.pu[:, 0:K]), p_u),
+                  lambda: vop(lambda: V.tensor_scalar(T.hb[:, 0:K], T.ha[:, 0:K], W - 1, None, A.bitwise_and), hl),
+                  lambda: vop(lambda: V.tensor_copy(T.ho[:, 0:K], T.hb[:, 0:K]), hl)][i]()
+            if i < 2:
+                next(side, None)
     if not first:
         ev_ue = vop(lambda: V.tensor_tensor(T.ue[:], T.pu[:, 0:K], land[0][:], A.add), p_u, ("ar0", n_in))
         need("s", DR0, DR2)
@@ -365,19 +375,24 @@ def rank_program(g, core, T, topo):
                     store("s", t, x0, x1)
             break
 
-        for b in range(2):
-            need("p", *gather((b, H, 2), T.ho[:, o + 16 * b:o + 16 * b + 16]))
+        for b in range(NC):
+            g_c, g_s = gather((b, NP // NC, NC), T.ho[:, o + K // NC * b:o + K // NC * (b + 1)])
+            rows = range(b, 16, NC)
             if not last:
-                p_v = hash_rows(T.pv, "v256", sm, 0, 2 * K, t == 1 and b == 0, b == 1, range(b, 16, 2))
-            if t < M - 1:
-                p_w = hash_rows(T.pw, "w256", sm, 0, K, False, b == 1, range(b, 16, 2))
+                need("p", g_c)
+                hash_rows(T.pv, "v256", sm, NP, K, t == 1 and b == 0, False, rows)
+                need("p", g_s)
+                p_v = hash_rows(T.pv, "v256", sm, 0, K, False, b == NC - 1, rows)
+            else:
+                need("p", g_s)
+                p_w = hash_rows(T.pw, "w256", sm, 0, K, False, b == NC - 1, rows)
+        need("p", g_c)
         if not last:
-            v_h = vop(lambda: V.tensor_copy(hp[:], T.pv[:, 0:2 * K]), p_v)
+            if t < M - 1:
+                p_w = hash_rows(T.pw, "w256", sm, 0, K, False, True)
+            v_h = vop(lambda: V.tensor_copy(hp[:, 0:K], T.pv[:, 0:K]), p_v)
             need("g", v_h)
-            g.remote_dma_fused([RemoteDMATransfer(
-                dst_ids=[DstId(rid=rid, pnc=pid)], dma_engine_mask=m_out, remote_sem=sem["ar%d" % t],
-                srcs=[hp[:, 0:K], hp[:, K:2 * K]], dsts=[land[t][:]], alu_op=1)],
-                local_sem=sem["sn%d" % t])
+            g.remote_dma(land[t][:], hp[:, 0:K], sem["ar%d" % t], sem["sn%d" % t], pid, rid, m_out)
         a_x = []
         for x0, x1, b in xparts(t):
             need("a", xsum(x0, x1, b))

from concourse.bass import DstId, RemoteDMATransfer
from concourse.mybir import AluOpType as A, ActivationFunctionType as F

W, S, M = 4096, 480, 4
PB = 9
NP = 1 << PB
K = NP // 16
K0 = S // 16
H = NP // 2
NB = 2
NC = 1 << NB
ZW, C0 = 144, 15
SC = [(0, 8), (8, 16), (16, 24), (24, 30)]
CH = [(0, 8), (8, 16), (16, 24), (24, 32)]
FIN = [(0, 12), (12, 22), (22, 30)]
TILES = {"w": (2, 1.0), "vn": (1, -1.0), "u": (0, 1.0), "wn": (2, -1.0),
         "v256": (1, 256.0), "w256": (2, 256.0)}

SCRATCH = {
    "tabw": ("sbuf", [128, W + 256], "bfloat16"),
    "rs": ("sbuf", [128, (M - 1) * S + NP], "bfloat16"),
    "hws": ("sbuf", [128, 3], "bfloat16"),
    "z": ("sbuf", [128, len(TILES) * ZW], "bfloat16"),
    "gm": ("sbuf", [128, 8], "bfloat16"),
    "idn": ("sbuf", [128, 128], "bfloat16"),
    "nidn": ("sbuf", [128, 128], "bfloat16"),
    "pi": ("sbuf", [128, 4], "int32"),
    "pf": ("sbuf", [128, 8], "float32"),
    "cb": ("sbuf", [128, 2 * K], "int32"),
    "base": ("sbuf", [128, 3 * K], "int32"),
    "nu": ("sbuf", [128, 24 * K], "int32"),
    "pl": ("sbuf", [128, 4 * K], "uint16"),
    "e0p": ("sbuf", [128, NP], "bfloat16"),
    "thr": ("sbuf", [128, 3 * NP], "bfloat16"),
    "xs": ("sbuf", [128, 3 * NP], "bfloat16"),
    "yb": ("sbuf", [128, 3 * NP], "bfloat16"),
    "e1s": ("sbuf", [128, K], "float32"),
    "ue": ("sbuf", [128, K], "float32"),
    "ha": ("sbuf", [128, 3 * K], "int32"),
    "hb": ("sbuf", [128, 3 * K], "int32"),
    "ho": ("sbuf", [128, 3 * K], "uint16"),
    "wa": ("sbuf", [128, 3 * K], "int32"),
    "wb": ("sbuf", [128, 3 * K], "int32"),
    "wc": ("sbuf", [128, 3 * K], "int32"),
    "wo": ("sbuf", [128, 3 * K], "uint16"),
    "land0": ("sbuf", [128, K], "float32"),
}
for _t in (1, 2, 3):
    SCRATCH["land%d" % _t] = ("sbuf", [128, K], "float32")
    SCRATCH["sm%d" % _t] = ("sbuf", [128, 2 * NP], "bfloat16")
    SCRATCH["hp%d" % _t] = ("sbuf", [128, 2 * K], "float32")
for _n in ("pv", "pw", "px0", "px1", "pu", "pe", "pf1", "pf2"):
    SCRATCH[_n] = ("psum", [128, 512], "float32")

SEMAPHORES = ["cv", "ca", "cp", "cg", "dr0", "dr1", "dr2", "dh", "dt0", "dt1", "dt2", "dt3", "dy",
              "ar0", "ar1", "ar2", "ar3", "sn0", "sn1", "sn2", "sn3"]


def relay_for(src, dst, T, topo):
    if topo.may_write(src, dst):
        return None
    cand = [c for c in topo.cores_of(src) if T.rank_of(c) is None and topo.may_write(c, dst)]
    cand.sort(key=lambda c: topo.die(c) != topo.die(src))
    return cand[0]


def nbits(m):
    return bin(m).count("1")


def hop_mask(src, dst, topo):
    return topo.mask(src, dst)


def span(start, count, step):
    return slice(start, start + (count - 1) * step + 1, step)


def pieces(level):
    s = NB * level % PB
    lo, hi = max(((0, s), (s, PB)), key=lambda r: r[1] - r[0])
    c = 1 << (hi - lo)
    return [(j, 1 << lo, (j >> s) | ((j << (PB - s)) & (NP - 1)), 1 << ((lo - s) % PB), c)
            for j in range(NP) if (j >> lo) & (c - 1) == 0]


def rank_program(g, core, T, topo):
    cores = list(T.cores)
    n = len(cores)
    rank = T.rank_of(core)
    sem = T.sem
    land = [T["land%d" % k] for k in range(4)]

    if rank is None:
        for r in range(n - 1):
            if relay_for(cores[r], cores[r + 1], T, topo) != core:
                continue
            dst = cores[r + 1]
            rid, pid = topo.addr(dst, core)
            m_in, m_out = hop_mask(cores[r], core, topo), hop_mask(core, dst, topo)
            for k in range(4):
                g.wait_ge(sem["ar%d" % k], nbits(m_in))
                g.remote_dma(land[k][:], land[k][:], sem["ar%d" % k], sem["sn%d" % k], pid, rid, m_out)
            for k in range(4):
                g.wait_ge(sem["sn%d" % k], nbits(m_out))
        return

    first, last = rank == 0, rank == n - 1
    Q = {"g": g, "v": g.vector, "a": g.scalar, "p": g.tensor, "s": g.sync}
    cnt = {"v": 0, "a": 0, "p": 0, "g": 0}
    seen = {}

    def done(q, inst):
        inst.then_inc(sem["c" + q], 1)
        cnt[q] += 1
        return ("c" + q, cnt[q])

    def need(q, *evs):
        for name, val in evs:
            if seen.get((q, name), 0) < val:
                Q[q].wait_ge(sem[name], val)
                seen[(q, name)] = val

    V, S_, P = g.vector, g.scalar, g.tensor

    def vop(inst_fn, *evs):
        need("v", *evs)
        return done("v", inst_fn())

    if not last:
        nxt = relay_for(core, cores[rank + 1], T, topo)
        nxt = cores[rank + 1] if nxt is None else nxt
        rid, pid = topo.addr(nxt, core)
        m_out = hop_mask(core, nxt, topo)
    if not first:
        prv = relay_for(cores[rank - 1], core, T, topo)
        prv = cores[rank - 1] if prv is None else prv
        n_in = nbits(hop_mask(prv, core, topo))

    g.sync.dma_start(T.rs[:, 0:S], T.res[:, 0:S]).then_inc(sem.dr0, 16)
    S_.dma_start(T.hws[:], T.hw[:]).then_inc(sem.dh, 16)
    if not first:
        S_.dma_start(T.rs[:, S:2 * S + 32], T.res[:, S:2 * S + 32]).then_inc(sem.dr1, 16)
        S_.dma_start(T.rs[:, 2 * S + 32:M * S], T.res[:, 2 * S + 32:M * S]).then_inc(sem.dr2, 16)
    for i, (c0, c1) in enumerate(CH):
        g.sync.dma_start(T.tabw[:, 128 * c0:128 * c1], T.tab[:, 128 * c0:128 * c1]).then_inc(sem["dt%d" % i], 16)
        if first and i == 0:
            g.sync.dma_start(T.rs[:, S:2 * S + 32], T.res[:, S:2 * S + 32]).then_inc(sem.dr1, 16)
    if first:
        g.sync.dma_start(T.rs[:, 2 * S + 32:M * S], T.res[:, 2 * S + 32:M * S]).then_inc(sem.dr2, 16)
    DR0, DR1, DR2, DH = ("dr0", 16), ("dr1", 16), ("dr2", 16), ("dh", 16)
    DT = ("dt%d" % (len(CH) - 1), 16)

    m_gm = done("v", V.memset(T.gm[:], 1.0))
    m_z = done("v", V.memset(T.z[:], 0.0))
    m_pad = done("v", V.memset(T.rs[:, M * S:(M - 1) * S + NP], 0.0))
    done("v", V.memset(T.idn[:], 256.0))
    m_id = done("v", V.memset(T.nidn[:], -1.0))
    i_p = done("g", g.iota(T.pi[:, 0:1], [[0, 1]], 0, 1))
    need("g", m_gm)
    s1 = done("g", g.affine_select(T.gm[:], T.gm[:], [[-16, 8]], A.is_ge, 0.0, 0, 1))
    done("g", g.iota(T.cb[:, 0:K], [[0, 4], [128, 8]], 0, 0))
    need("g", s1)
    s_gm = done("g", g.affine_select(T.gm[:], T.gm[:], [[16, 8]], A.is_ge, 0.0, 15, -1))
    i_cb = done("g", g.iota(T.cb[:, K:2 * K], [[16, K]], 0, 0))
    need("g", m_id)
    for t_id in (T.nidn, T.idn):
        s_id = done("g", g.affine_select(t_id[:], t_id[:], [[-1, 128]], A.is_equal, 0.0, 0, 1))

    A1, A8 = T.pf[:, 0:1], T.pf[:, 1:2]
    e = vop(lambda: V.tensor_scalar(T.pi[:, 1:2], T.pi[:, 0:1], 15, None, A.bitwise_and), i_p)
    vop(lambda: V.tensor_copy(A1, T.pi[:, 1:2]), e)
    e8 = vop(lambda: V.tensor_scalar(A8, T.pi[:, 1:2], 8.0, None, A.mult))
    k_base0 = vop(lambda: V.tensor_scalar(T.base[:, 0:K0], T.cb[:, 0:K0], A8, None, A.add), e8, i_cb)
    kev = {}

    def orders():
        nu = [T.nu[:, 4 * K * i:4 * K * (i + 1)] for i in range(6)]
        for i, t in enumerate((1, 2, 3, 0)):
            e = vop(lambda: V.tensor_scalar(T.nu[:, K * i:K * (i + 1)], T.cb[:, K:2 * K], A1,
                                            float(1 << (PB - NB * (rank + t) % PB)), A.add, A.mult))
        yield
        vop(lambda: V.tensor_scalar(nu[1], nu[0], NP - 1, None, A.bitwise_and), e)
        e = vop(lambda: V.tensor_scalar(nu[2], nu[0], PB, None, A.logical_shift_right))
        yield
        e = vop(lambda: V.tensor_tensor(nu[3], nu[1], nu[2], A.add), e)
        yield
        kev["list"] = vop(lambda: V.tensor_copy(T.pl[:], nu[3]), e)
        vop(lambda: V.tensor_scalar(nu[4], nu[3], 8.0, None, A.mult))
        e = vop(lambda: V.tensor_scalar(nu[5], nu[3], float(S), 256.0, A.is_ge, A.mult))
        yield
        kev["base"] = vop(lambda: V.tensor_tensor(T.base[:, K:3 * K], T.nu[:, 16 * K:18 * K], T.nu[:, 20 * K:22 * K],
                                                  A.add), e)

    side = orders()
    if not first:
        for _ in side:
            pass

    zev = {}

    def fill(names):
        for name in names:
            col, scale = TILES[name]
            if not (last and col == 1):
                c = list(TILES).index(name) * ZW + C0
                zev[name] = vop(lambda: V.tensor_scalar(T.z[:, span(c, 8, 16)], T.gm[:], T.hws[:, col:col + 1],
                                                        scale, A.mult, A.mult), m_z, s_gm, DH)

    fill(list(TILES))
    next(side, None)
    next(side, None)

    def tile(name, row):
        c = list(TILES).index(name) * ZW + C0 - row
        return T.z[:, c:c + 128]

    def hash_rows(out, name, buf, c0, cols, start, stop, rows=range(16)):
        need("p", zev[name])
        for a in rows:
            inst = P.matmul(out[:, 0:cols], tile(name, a), buf[:, span(c0 + a, cols, 16)],
                            start and a == rows[0], stop and a == rows[-1])
        return done("p", inst) if stop else None

    def xparts(t):
        if last and t == M - 1:
            return [(16 * c0, 16 * c1, b) for (c0, c1), b in zip(FIN, (T.pe, T.pf1, T.pf2))]
        return [(0, H, T.px0), (H, NP, T.px1)]

    def pre(t):
        need("p", thr[t], s_id)
        if t > 1 and not last:
            hash_rows(T.pv, "vn", T.thr, (t - 1) * NP, K, True, False)
        if t < M - 1:
            hash_rows(T.pw, "wn", T.thr, (t - 1) * NP, K, True, False)
        for x0, x1, b in xparts(t):
            P.matmul(b[:, 0:x1 - x0], T.nidn[:], T.thr[:, (t - 1) * NP + x0:(t - 1) * NP + x1], True, False)

    def order(t):
        i = (t - 1) % M
        return T.pl[:, K * i:K * (i + 1)]

    def permute(out, o0, i0, level, bias, scale):
        if len(pieces(level)) > 4:
            need("a", kev["list"], DR2, m_pad)
            return done("a", S_.activation(out[:, o0:o0 + NP], T.rs[:, i0:i0 + NP].indirect(order(level - rank)),
                                           F.Identity, bias, scale))
        for j, sj, s, ss, c in pieces(level):
            inst = S_.activation(out[:, span(o0 + j, c, sj)], T.rs[:, span(i0 + s, c, ss)], F.Identity, bias, scale)
        return done("a", inst)

    def make_thr(t):
        need("a", DR1, *([DR2, m_pad] if t > 1 else []))
        level = 0 if last and t == M - 1 else rank + t
        return permute(T.thr, (t - 1) * NP, t * S, level, 256.0, -1.0)

    def wlist(t, bank, ev, cols):
        o = K * t
        e0 = vop(lambda: V.tensor_copy(T.wa[:, o:o + cols], bank[:, 0:cols]), ev)
        next(side, None)
        e = vop(lambda: V.tensor_scalar(T.wb[:, o:o + cols], T.wa[:, o:o + cols], 7, None, A.bitwise_and), e0)
        next(side, None)
        e = vop(lambda: V.tensor_tensor(T.wc[:, o:o + cols], T.wb[:, o:o + cols], T.base[:, o:o + cols], A.add), e)
        next(side, None)
        return e0, vop(lambda: V.tensor_copy(T.wo[:, o:o + cols], T.wc[:, o:o + cols]), e)

    def hlist(t, ev):
        o = K * (t - 1)
        e = vop(lambda: V.tensor_scalar(T.hb[:, o:o + K], T.ha[:, o:o + K], W - 1, None, A.bitwise_and), ev)
        return vop(lambda: V.tensor_copy(T.ho[:, o:o + K], T.hb[:, o:o + K]), e)

    ny = [0]

    def store(q, t, c0, c1):
        natural = (rank + t) % PB == 0 or (last and t == M - 1)
        src = T.rs[:, c0:c1] if t == 0 else (T.xs if natural else T.yb)[:, (t - 1) * NP + c0:(t - 1) * NP + c1]
        Q[q].dma_start(T.y[:, t * S + c0:t * S + c1], src).then_inc(sem.dy, 16)
        ny[0] += 16

    def unpermute(q, t):
        tb = (t - 1) * NP
        if (rank + t) % PB == 0:
            return ev_x[t]
        need(q, ev_x[t])
        if len(pieces(rank + t)) > 8:
            return vop(lambda: V.tensor_copy(T.yb[:, tb:tb + NP].indirect(order(t)), T.xs[:, tb:tb + NP]))
        for j, sj, s, ss, c in pieces(rank + t):
            out, src = T.yb[:, span(tb + s, c, ss)], T.xs[:, span(tb + j, c, sj)]
            inst = V.tensor_copy(out, src) if q == "v" else S_.activation(out, src, F.Identity)
        return done(q, inst)

    need("p", DR0)
    p_w = hash_rows(T.pf1, "w", T.rs, 0, K0, True, True)
    thr = {1: make_thr(1)}
    if not first:
        need("a", DR0)
        a_e0 = permute(T.e0p, 0, 0, rank, 0.0, 1.0)
    if first:
        need("p", DR1)
        p_u = hash_rows(T.pu, "u", T.rs, 0, K, True, True)
    need("p", thr[1])
    if not last:
        p_e = hash_rows(T.pe, "vn", T.thr, 0, K, True, True)
        need("a", p_e)
        a_e1 = done("a", S_.activation(T.e1s[:], T.pe[:, 0:K], F.Identity))
        need("g", a_e1)
        g.remote_dma(land[0][:], T.e1s[:], sem.ar0, sem.sn0, pid, rid, m_out)
    if not first:
        need("p", a_e0)
        p_u = hash_rows(T.pu, "u", T.e0p, 0, K, True, True)
    pre(1)
    if not first:
        for t in (2, 3):
            thr[t] = make_thr(t)

    v_w, wl = wlist(0, T.pf1, p_w, K0)
    for i, (c0, c1) in enumerate(SC):
        sc = vop(lambda: V.tensor_copy(T.tabw[:, 128 * c0:128 * c1].indirect(T.wo[:, c0:c1]),
                                       T.rs[:, 16 * c0:16 * c1]), wl, ("dt%d" % i, 16))
        if first and i < 3:
            hl = [lambda: vop(lambda: V.tensor_copy(T.ha[:, 0:K], T.pu[:, 0:K]), p_u),
                  lambda: vop(lambda: V.tensor_scalar(T.hb[:, 0:K], T.ha[:, 0:K], W - 1, None, A.bitwise_and), hl),
                  lambda: vop(lambda: V.tensor_copy(T.ho[:, 0:K], T.hb[:, 0:K]), hl)][i]()
            if i < 2:
                next(side, None)
    if not first:
        ev_ue = vop(lambda: V.tensor_tensor(T.ue[:], T.pu[:, 0:K], land[0][:], A.add), p_u, ("ar0", n_in))
        need("s", DR0, DR2)
        store("s", 0, 0, S)

    table = T.tabw[:, 0:W]
    ev_x = {}

    for t in range(1, M):
        o = K * (t - 1)
        sm, hp = T["sm%d" % t], T["hp%d" % t]
        tb = (t - 1) * NP
        if first:
            if t > 1:
                hl = hlist(t, vop(lambda: V.tensor_copy(T.ha[:, o:o + K], T.pu[:, 0:K]), p_u))
        elif t == 1:
            hl = hlist(t, vop(lambda: V.tensor_tensor(T.ha[:, o:o + K], T.ue[:], land[t][:], A.add),
                              ev_ue, ("ar1", n_in)))
        else:
            hl = hlist(t, vop(lambda: V.tensor_tensor(T.ha[:, o:o + K], T.pu[:, 0:K], land[t][:], A.add),
                              p_u, ("ar%d" % t, n_in)))

        def gather(places, offs):
            c0, count, step = places
            g_c = vop(lambda: V.tensor_tensor(sm[:, span(NP + c0, count, step)], table.indirect(offs),
                                              T.thr[:, span(tb + c0, count, step)], A.is_lt), hl, sc, thr[t], DT)
            need("a", hl, sc, DT)
            g_s = done("a", S_.activation(sm[:, span(c0, count, step)], table.indirect(offs), F.Identity,
                                          0.0, 1.0 / 256.0))
            return g_c, g_s

        def xsum(x0, x1, b):
            P.matmul(b[:, 0:x1 - x0], T.idn[:], sm[:, x0:x1], False, False)
            return done("p", P.matmul(b[:, 0:x1 - x0], T.idn[:], sm[:, NP + x0:NP + x1], False, True))

        if last and t == M - 1:
            p_x = []
            for x0, x1, b in xparts(t):
                need("p", *gather((x0, x1 - x0, 1), T.ho[:, o + x0 // 16:o + x1 // 16]))
                p_x.append(xsum(x0, x1, b))
            for i, (x0, x1, b) in enumerate(xparts(t)):
                if i == 1:
                    need("a", p_x[i])
                    e = done("a", S_.activation(T.xs[:, tb + x0:tb + x1], b[:, 0:x1 - x0], F.Identity))
                    need("a", e)
                    store("a", t, x0, x1)
                else:
                    e = vop(lambda: V.tensor_copy(T.xs[:, tb + x0:tb + x1], b[:, 0:x1 - x0]), p_x[i])
                    need("s", e)
                    store("s", t, x0, x1)
            break

        for b in range(NC):
            g_c, g_s = gather((b, NP // NC, NC), T.ho[:, o + K // NC * b:o + K // NC * (b + 1)])
            rows = range(b, 16, NC)
            if not last:
                need("p", g_c)
                hash_rows(T.pv, "v256", sm, NP, K, t == 1 and b == 0, False, rows)
                need("p", g_s)
                p_v = hash_rows(T.pv, "v256", sm, 0, K, False, b == NC - 1, rows)
            else:
                need("p", g_s)
                p_w = hash_rows(T.pw, "w256", sm, 0, K, False, b == NC - 1, rows)
        need("p", g_c)
        if not last:
            if t < M - 1:
                p_w = hash_rows(T.pw, "w256", sm, 0, K, False, True)
            v_h = vop(lambda: V.tensor_copy(hp[:, 0:K], T.pv[:, 0:K]), p_v)
            need("g", v_h)
            g.remote_dma(land[t][:], hp[:, 0:K], sem["ar%d" % t], sem["sn%d" % t], pid, rid, m_out)
        a_x = []
        for x0, x1, b in xparts(t):
            need("a", xsum(x0, x1, b))
            a_x.append(done("a", S_.activation(T.xs[:, tb + x0:tb + x1], b[:, 0:x1 - x0], F.Identity)))
        ev_x[t] = a_x[-1]

        if t == M - 1:
            need("s", ("sn3", nbits(m_out)))
            if first:
                store("s", 0, 0, S)
            for u in range(1, M):
                need("s", unpermute("v", u))
                store("s", u, 0, S)
            break

        v_w, wl = wlist(t, T.pw, p_w, K)
        sc = vop(lambda: V.tensor_copy(T.tabw[:].indirect(T.wo[:, K * t:K * (t + 1)]), T.xs[:, tb:tb + NP]),
                 wl, ev_x[t])
        need("p", ev_x[t])
        p_u = hash_rows(T.pu, "u", T.xs, tb, K, True, True)
        if first:
            thr[t + 1] = make_thr(t + 1)
        need("p", v_w)
        pre(t + 1)
        if last:
            need("s", unpermute("a", t))
            store("s", t, 0, S)

    need("s", ("dy", ny[0]))
    for q in ("v", "a", "p", "g"):
        need("g", ("c" + q, cnt[q]))
    if not last:
        for k in range(4):
            need("g", ("sn%d" % k, nbits(m_out)))
